import numpy as np
import ml_dtypes


def mxq(x, axis, fmt="e4m3"):
    dtype, down = {"e4m3": (ml_dtypes.float8_e4m3fn, 7), "e5m2": (ml_dtypes.float8_e5m2, 14)}[fmt]
    v = np.moveaxis(np.asarray(x, np.float32).astype(ml_dtypes.bfloat16).astype(np.float64), axis, -1)
    blocks = v.reshape(v.shape[:-1] + (-1, 32))
    amax = np.abs(blocks).max(-1, keepdims=True)
    byte = np.maximum(np.where(amax > 0, np.frexp(amax)[1] - 1 + 127, 0) - down, 1)
    scale = np.exp2(byte - 127.0)
    codes = (blocks / scale).astype(np.float32).astype(dtype).astype(np.float64)
    return np.moveaxis((codes * scale).reshape(v.shape), -1, axis)


WIDE = False


def mx_kscale(k):
    if not WIDE:
        return np.ones(k)
    levels = np.array([10, -10, 5, -5, 0])
    if k % 512:
        return np.exp2(np.random.permutation(np.resize(levels, k // 32))).repeat(32)
    a = np.empty((k // 512, 16))
    for p in range(k // 512):
        a[p, :8] = np.random.permutation(np.resize(levels, 8))
        for g in range(8):
            far = levels[np.abs(levels - a[p, g]) >= 10]
            a[p, g + 8] = far[np.random.randint(len(far))]
    return np.exp2(a.ravel()).repeat(32)


BF16 = ml_dtypes.bfloat16


def bf(x):
    return np.asarray(x, np.float32).astype(BF16)


def f64(x):
    return np.asarray(x).astype(np.float64)


E2M1 = np.array([0.0, 0.5, 1.0, 1.5, 2.0, 3.0, 4.0, 6.0, -0.0, -0.5, -1.0, -1.5, -2.0, -3.0, -4.0, -6.0])


def pack_weight(w, fmt):
    k, n = w.shape
    w = f64(bf(w)).reshape(k // 32, 32, n)
    amax = np.abs(w).max(1)
    if fmt == "e4m3":
        byte = np.frexp(amax)[1] - 1 + 127 - 7
    else:
        mant, ex = np.frexp(amax / 6.0)
        byte = np.where(mant > 0.5, ex, ex - 1) + 127
    byte = np.clip(np.where(amax > 0, byte, 1), 1, 254)
    scaled = (w * np.exp2(127.0 - byte)[:, None, :]).reshape(k, n).astype(np.float32)
    by_word = np.ascontiguousarray(scaled.reshape(k // 512, 128, 4, n).transpose(0, 1, 3, 2))
    if fmt == "e4m3":
        words = by_word.astype(ml_dtypes.float8_e4m3fn).view(np.uint8)
    else:
        c = by_word.astype(ml_dtypes.float4_e2m1fn).view(np.uint8) & 0xF
        words = c[..., 0::2] | (c[..., 1::2] << 4)
    return np.ascontiguousarray(words), np.ascontiguousarray(byte.astype(np.uint8).reshape(k // 512, 16, n))


def unpack_weight(words, scales, fmt):
    g, p, n, _ = words.shape
    if fmt == "e4m3":
        vals = np.ascontiguousarray(words).view(ml_dtypes.float8_e4m3fn).astype(np.float64)
    else:
        nib = np.empty((g, p, n, 4), np.uint8)
        nib[..., 0::2] = words & 0xF
        nib[..., 1::2] = words >> 4
        vals = E2M1[nib]
    vals = vals * np.repeat(np.exp2(scales.astype(np.float64) - 127.0), 8, axis=1)[..., None]
    return vals.transpose(0, 1, 3, 2).reshape(g * 512, n)
def pack4(w):
    words, scales = pack_weight(w, "e2m1")
    return words.reshape(words.shape[0], 128, -1), scales


def unpack4(words, scales):
    return unpack_weight(words.reshape(words.shape[0], 128, -1, 2), scales, "e2m1")


def planes(Y):
    n, m = Y.shape
    b = f64(bf(Y)).reshape(n // 32, 32, m)
    amax = np.abs(b).max(1)
    byte = np.clip(np.where(amax > 0, np.frexp(amax)[1] - 1 + 127 - 7, 1), 1, 254)
    codes = (b * np.exp2(127.0 - byte)[:, None, :]).reshape(n, m).astype(np.float32).astype(ml_dtypes.float8_e4m3fn).view(np.uint8)
    words = codes.reshape(n // 512, 128, 4, m).transpose(0, 1, 3, 2)
    return np.ascontiguousarray(words), np.ascontiguousarray(byte.astype(np.uint8).reshape(n // 512, 16, m))


R, K, NA, NB = 2048, 1024, 512, 1024


def setup_inputs():
    s = mx_kscale(K)
    t = mx_kscale(R)
    rnd = np.random.standard_normal
    prim = rnd((K, R)) * s[:, None]
    prim_words, prim_scales = pack_weight(prim, "e4m3")
    coef_a = rnd((K, NA)) / np.sqrt(K) / s[:, None]
    coef_a_words, coef_a_scales = pack4(coef_a)
    spread = np.exp(0.8 * rnd(NB))
    coef_b = bf(rnd((K, NB)) * spread[None, :] / np.sqrt(K) / s[:, None])
    quad = bf(np.exp(0.4 * rnd(R)) / R ** 0.25 * t)
    vxc = bf(-np.exp(0.4 * rnd(R)) / R ** 0.25 / t)
    h_rest = bf(rnd((NA, NB)) * spread[None, :])
    return {"prim_words": prim_words, "prim_scales": prim_scales,
            "coef_a_words": coef_a_words, "coef_a_scales": coef_a_scales,
            "coef_b": coef_b, "quad": quad, "vxc": vxc, "h_rest": h_rest}


def reference(prim_words, prim_scales, coef_a_words, coef_a_scales, coef_b, quad, vxc, h_rest):
    prim = unpack_weight(prim_words, prim_scales, "e4m3")
    coef_a = unpack4(coef_a_words, coef_a_scales)
    phi_a = prim.T @ coef_a
    phi_b = prim.T @ mxq(f64(coef_b), 0, "e4m3")
    left = phi_a * f64(quad)[:, None]
    right = phi_b * f64(vxc)[:, None]
    y = (mxq(left, 0, "e4m3").T @ mxq(right, 0, "e4m3")) + f64(h_rest)
    Y = y.T
    words, scales = planes(Y)
    return y, words, scales

@@ -1,0 +1,255 @@
+from contextlib import ExitStack
+
+import concourse.mybir as mybir
+from concourse.masks import make_identity
+
+R, K, NA, NB = 2048, 1024, 512, 1024
+FLOPS = 2 * R * K * (NA + NB) + 2 * R * NA * NB
+
+F32 = mybir.dt.float32
+BF16 = mybir.dt.bfloat16
+I32 = mybir.dt.int32
+U8 = mybir.dt.uint8
+FP8X4 = mybir.dt.float8_e4m3fn_x4
+FP4X4 = mybir.dt.float4_e2m1fn_x4
+COPY = mybir.ActivationFunctionType.Copy
+ADD = mybir.AluOpType.add
+
+P = 128
+W = 512
+
+ORDER = """
+PP0 SP01 UU000 PP1 SP14 UU014 CV00 CV01 CQ00 CQ01 UU100 PP2 IV00 UU114 PP3 QQ00 UU020 IV01 IV10 QQ01 QQ10 UU124 CV10 CV11 CQ10 CQ11 UU030
+IV11 IV02 QQ11 QQ02 UU134 IV12 IV03 QQ12 QQ03 UU200 UU214 IV13 IV20 QQ13 QQ20 UU220 UU234 IV21 IV22 QQ21 QQ22 YY00004 YY10104 IV23 AD000 QQ23 AD101 YY20204 YY30304 CA00 CA10 
+AD202 AD303 CA20 CA30 YY01404 TT0200 CO0200 YY11504 AD014 CA01 TT2401 CO2401 OQ020 AD115 CA11 YY21604 OQ240 AD216 CA21 YY31704 TT0212 CO0212 TT2313 AB317 CO2313 TT3410 CO3410 AD317 OQ021 OQ231 OQ341
+""".split()
+
+
+def tile_exchange_correlation_block_k4_kernel(
+    tc, prim_words, prim_scales, coef_a_words, coef_a_scales, coef_b, quad, vxc, h_rest, out_0, out_1, out_2
+):
+    nc = tc.nc
+    with ExitStack() as ctx:
+        keep = ctx.enter_context(tc.tile_pool(name="keep", bufs=1))
+        psum = ctx.enter_context(tc.psum_pool(name="psum", bufs=1))
+        ctx.enter_context(tc.manual_schedule())
+
+        def sb(name, shape, dtype):
+            return keep.tile(shape, dtype, name=name, align_bytes=64)
+
+        banks = [psum.tile([P, W], F32, name="bank%d" % b) for b in range(8)]
+        p_raw = [sb("p_raw%d" % G, [P, 2, W], I32) for G in range(4)]
+        p_perm = [sb("p_perm%d" % G, [P, 4, 2, P], I32) for G in range(4)]
+        ps_raw = sb("ps_raw", [P, 2, R // 4], I32)
+        ps_perm = sb("ps_perm", [P, 4, 2, R // 16], I32)
+        ca_words = sb("ca_words", [P, 2, 2 * NA], U8)
+        ca_scales = sb("ca_scales", [P, 2, NA], U8)
+        cb_raw = {(h, g): sb("cb_raw%d%d" % (h, g), [P, 4, W], BF16) for h in range(2) for g in range(2)}
+        cb_grp = {(h, g): sb("cb_grp%d%d" % (h, g), [P, W, 4], BF16) for h in range(2) for g in range(2)}
+        cb_codes = {(h, g): sb("cb_codes%d%d" % (h, g), [P, W], I32) for h in range(2) for g in range(2)}
+        cb_scales = {(h, g): sb("cb_scales%d%d" % (h, g), [P, W], U8) for h in range(2) for g in range(2)}
+        h_sb = [sb("h_sb%d" % h, [P, 4, W], BF16) for h in range(2)]
+        fac_raw = sb("fac_raw", [8, W], BF16)
+        fac_rows = sb("fac_rows", [P, W], F32)
+        fac = sb("fac", [P, 4, 8], F32)
+        ident = sb("ident", [P, P], F32)
+        units = [(c, G) for c in range(3) for G in range(4)]
+        rows = {u: sb("rows%d%d" % u, [P, 4, W], BF16) for u in units}
+        grp_ring = [sb("grp%d" % n, [P, W, 4], BF16) for n in range(4)]
+        turns = [s for s in ORDER if s[0] == "I"]
+        grp = {(int(s[2]), int(s[3])): grp_ring[n % 4] for n, s in enumerate(turns)}
+        codes = {u: sb("codes%d%d" % u, [P, W], I32) for u in units}
+        scales = {u: sb("scales%d%d" % u, [P, W], U8) for u in units}
+        y_sb = {(i, h): sb("y%d%d" % (i, h), [P, W], F32) for i in range(4) for h in range(2)}
+        y_bf = {(i, h): sb("ybf%d%d" % (i, h), [P, W], BF16) for i in range(4) for h in range(2)}
+        o_grp = [sb("o_grp%d" % h, [P, W, 4], BF16) for h in range(2)]
+        o_codes = [sb("o_codes%d" % h, [P, W], I32) for h in range(2)]
+        o_scales = [sb("o_scales%d" % h, [P, W], U8) for h in range(2)]
+
+        nc.vector.memset(ps_raw[:], 0)
+        nc.vector.memset(ca_scales[:].rearrange("p g n -> p (g n)").bitcast(I32), 0)
+        nc.gpsimd.dma_start(out=fac_raw[0:4, :], in_=quad.rearrange("(G n) -> G n", G=4))
+        nc.gpsimd.dma_start(out=fac_raw[4:8, :], in_=vxc.rearrange("(G n) -> G n", G=4))
+        nc.gpsimd.memset(fac_rows[:], 0.0)
+        make_identity(nc, ident[:])
+
+        pw = prim_words.rearrange("g p n t -> p g (n t)").bitcast(I32)
+        psc = prim_scales.rearrange("g q n -> q g n").bitcast(I32)
+        cas = coef_a_scales.rearrange("g q n -> q g n").bitcast(I32)
+
+        def load_p(G):
+            nc.sync.dma_start(out=p_raw[G][:], in_=pw[:, :, G * W : (G + 1) * W])
+
+        def load_cb(h, g):
+            src = coef_b[g * W : (g + 1) * W, h * W : (h + 1) * W]
+            nc.sync.dma_start(out=cb_raw[h, g][:], in_=src.rearrange("(p j) n -> p j n", j=4))
+
+        nc.sync.dma_start(out=ca_words[:].bitcast(I32), in_=coef_a_words.rearrange("g p n -> p g n").bitcast(I32))
+        load_p(0)
+        for Q in range(4):
+            nc.sync.dma_start(out=ps_raw[32 * Q : 32 * Q + 4, :, :], in_=psc[4 * Q : 4 * Q + 4, :, :])
+        for Q in range(4):
+            nc.sync.dma_start(
+                out=ca_scales[32 * Q : 32 * Q + 4, :, :].bitcast(I32), in_=cas[4 * Q : 4 * Q + 4, :, :]
+            )
+        load_p(1)
+        load_cb(0, 0)
+        load_cb(0, 1)
+        load_p(2)
+        load_p(3)
+        load_cb(1, 0)
+        load_cb(1, 1)
+        for h in range(2):
+            src = h_rest[:, h * W : (h + 1) * W]
+            nc.sync.dma_start(out=h_sb[h][:], in_=src.rearrange("(a p) j -> p a j", p=P))
+
+        nc.scalar.activation(
+            out=fac_rows[0:8, :].rearrange("v (t q e) -> v t q e", t=4, e=8),
+            in_=fac_raw[:].rearrange("v (q t e) -> v t q e", t=4, e=8),
+            func=COPY,
+        )
+        for t in range(4):
+            nc.tensor.transpose(banks[7][:, t * P : (t + 1) * P], fac_rows[:, t * P : (t + 1) * P], ident[:])
+        nc.scalar.activation(out=fac[:], in_=banks[7][:].rearrange("p (t v) -> p t v", t=4)[:, :, 0:8], func=COPY)
+
+        def permute_words(G):
+            nc.vector.tensor_copy(
+                out=p_perm[G][:].rearrange("p t g (q e) -> p t (g q) e", e=8),
+                in_=p_raw[G][:].rearrange("p g (q t e) -> p t (g q) e", t=4, e=8),
+            )
+
+        def permute_scales(G0, G1):
+            for g in range(2):
+                nc.vector.tensor_copy(
+                    out=ps_perm[:, :, g, 32 * G0 : 32 * G1].rearrange("p t (b e) -> p t b e", e=2),
+                    in_=ps_raw[:, g, P * G0 : P * G1].rearrange("p (b t e) -> p t b e", t=4, e=2),
+                )
+
+        def interleave(engine, dst, src):
+            out = dst[:].rearrange("p (c i) t -> p c t i", i=4)
+            in_ = src[:].rearrange("p t (c i) -> p c t i", i=4)
+            if engine == "V":
+                nc.vector.tensor_copy(out=out, in_=in_)
+            else:
+                nc.scalar.copy(out=out, in_=in_)
+
+        def quantize(dst, sc, src, c0, c1):
+            nc.vector.quantize_mx(
+                out=dst[:, c0:c1].bitcast(FP8X4),
+                scales=sc[:, c0:c1],
+                in_=src[:, c0:c1, :].rearrange("p w j -> p (w j)"),
+            )
+
+        def stage1(c, G, b0):
+            for t in range(4):
+                bank = banks[(b0 + t) % 8]
+                for g in range(2):
+                    if c == 0:
+                        rhs = ca_words[:, g, :].bitcast(FP4X4)
+                        rhs_scale = ca_scales[:, g, :]
+                    else:
+                        rhs = cb_codes[c - 1, g][:].bitcast(FP8X4)
+                        rhs_scale = cb_scales[c - 1, g][:]
+                    nc.tensor.matmul_mx(
+                        out=bank[:],
+                        lhsT=p_perm[G][:, t, g, :].bitcast(FP8X4),
+                        lhsT_scale=ps_perm[:, t, g, 32 * G : 32 * (G + 1)].bitcast(U8),
+                        rhs=rhs,
+                        rhs_scale=rhs_scale,
+                        start=(g == 0),
+                        stop=(g == 1),
+                    )
+                v = G if c == 0 else 4 + G
+                nc.scalar.activation(out=rows[c, G][:, t, :], in_=bank[:], func=COPY, scale=fac[:, t, v : v + 1])
+
+        def stage2(i, h, b, G0, G1):
+            for G in range(G0, G1):
+                nc.tensor.matmul_mx(
+                    out=banks[b][:],
+                    lhsT=codes[0, G][:, i * P : (i + 1) * P].bitcast(FP8X4),
+                    lhsT_scale=scales[0, G][:, i * P : (i + 1) * P],
+                    rhs=codes[1 + h, G][:].bitcast(FP8X4),
+                    rhs_scale=scales[1 + h, G][:],
+                    start=(G == 0),
+                    stop=(G == 3),
+                )
+
+        def add_rest(i, h, b):
+            nc.vector.tensor_tensor(out=y_sb[i, h][:], in0=banks[b][:], in1=h_sb[h][:, i, :], op=ADD)
+            nc.sync.dma_start(out=out_0[i * P : (i + 1) * P, h * W : (h + 1) * W], in_=y_sb[i, h][:])
+
+        def add_round(i, h, b):
+            nc.vector.tensor_tensor(
+                out=y_bf[i, h][:].rearrange("p (u m e) -> p u m e", u=2, e=2),
+                in0=banks[b][:].rearrange("p (m u e) -> p u m e", u=2, e=2),
+                in1=h_sb[h][:, i, :].rearrange("p (m u e) -> p u m e", u=2, e=2),
+                op=ADD,
+            )
+
+        def cast(i, h):
+            nc.scalar.copy(
+                out=y_bf[i, h][:].rearrange("p (u m e) -> p u m e", u=2, e=2),
+                in_=y_sb[i, h][:].rearrange("p (m u e) -> p u m e", u=2, e=2),
+            )
+
+        def turn(i0, i1, h, b):
+            for i in range(i0, i1):
+                words = y_bf[i, h][:].bitcast(F32)
+                for u in range(2):
+                    s = 2 * (i - i0) + u
+                    nc.tensor.transpose(banks[b][:, s * P : (s + 1) * P], words[:, u * P : (u + 1) * P], ident[:])
+
+        def copy_out(i0, i1, h, b):
+            n = i1 - i0
+            dst = o_grp[h][:, i0 * P : i1 * P, :].rearrange("p m t -> p (m t)").bitcast(F32)
+            nc.scalar.copy(
+                out=dst.rearrange("p (a m u) -> p a m u", a=n, u=2),
+                in_=banks[b][:, 0 : 2 * n * P].rearrange("p (a u m) -> p a m u", a=n, u=2),
+            )
+
+        def out_quant(i0, i1, h):
+            quantize(o_codes[h], o_scales[h], o_grp[h], i0 * P, i1 * P)
+            dst = out_1[h].rearrange("p m t -> p (m t)").bitcast(I32)
+            nc.sync.dma_start(out=dst[:, i0 * P : i1 * P], in_=o_codes[h][:, i0 * P : i1 * P])
+            if i1 == 4:
+                for Q in range(4):
+                    nc.sync.dma_start(
+                        out=out_2[h, 4 * Q : 4 * Q + 4, :].bitcast(I32),
+                        in_=o_scales[h][32 * Q : 32 * Q + 4, :].bitcast(I32),
+                    )
+
+        for step in ORDER:
+            kind = step[0:2]
+            a = [int(ch) for ch in step[2:]]
+            if kind == "PP":
+                permute_words(a[0])
+            elif kind == "SP":
+                permute_scales(a[0], a[1])
+            elif kind == "CV":
+                interleave("V", cb_grp[a[0], a[1]], cb_raw[a[0], a[1]])
+            elif kind == "CS":
+                interleave("S", cb_grp[a[0], a[1]], cb_raw[a[0], a[1]])
+            elif kind == "CQ":
+                quantize(cb_codes[a[0], a[1]], cb_scales[a[0], a[1]], cb_grp[a[0], a[1]], 0, W)
+            elif kind == "UU":
+                stage1(a[0], a[1], a[2])
+            elif kind == "IV":
+                interleave("V", grp[a[0], a[1]], rows[a[0], a[1]])
+            elif kind == "IS":
+                interleave("S", grp[a[0], a[1]], rows[a[0], a[1]])
+            elif kind == "QQ":
+                quantize(codes[a[0], a[1]], scales[a[0], a[1]], grp[a[0], a[1]], 0, W)
+            elif kind == "YY":
+                stage2(a[0], a[1], a[2], a[3], a[4])
+            elif kind == "AD":
+                add_rest(a[0], a[1], a[2])
+            elif kind == "AB":
+                add_round(a[0], a[1], a[2])
+            elif kind == "CA":
+                cast(a[0], a[1])
+            elif kind == "TT":
+                turn(a[0], a[1], a[2], a[3])
+            elif kind == "CO":
+                copy_out(a[0], a[1], a[2], a[3])
+            else:
+                out_quant(a[0], a[1], a[2])

@@ -17,11 +17,10 @@ ADD = mybir.AluOpType.add
 
 P = 128
 W = 512
+WARM = (14, 8)
 
 ORDER = """
-PP0 SP01 UU000 PP1 SP14 UU014 CV00 CV01 CQ00 CQ01 UU100 PP2 IV00 UU114 PP3 QQ00 UU020 IV01 IV10 QQ01 QQ10 UU124 CV10 CV11 CQ10 CQ11 UU030
-IV11 IV02 QQ11 QQ02 UU134 IV12 IV03 QQ12 QQ03 UU200 UU214 IV13 IV20 QQ13 QQ20 UU220 UU234 IV21 IV22 QQ21 QQ22 YY00004 YY10104 IV23 AD000 QQ23 AD101 YY20204 YY30304 CA00 CA10 
-AD202 AD303 CA20 CA30 YY01404 TT0200 CO0200 YY11504 AD014 CA01 TT2401 CO2401 OQ020 AD115 CA11 YY21604 OQ240 AD216 CA21 YY31704 TT0212 CO0212 TT2313 AB317 CO2313 TT3410 CO3410 AD317 OQ021 OQ231 OQ341
+PP0 SP02 CS000 CV001 PP1 UU000123 CQ00 CV012 CQ01 PP2 SP24 PP3 CV102 CV112 UU014567 IV012 IV002 UU110123 CQ10 UU034567 QQ00 UU100123 UU124567 UU020123 IV032 IV112 QQ01 UU134567 QQ03 CQ11 IV122 UU210123 IV022 UU204567 QQ11 UU230123 QQ12 IV132 IV102 QQ02 QQ10 IV202 QQ13 UU224567 IV212 QQ20 YY10004 IV222 YY00104 QQ21 IS232 QQ22 QQ23 YY20204 YY30304 AD100 YY21404 AD202 CA20 AD303 CA10 YY01504 AD214 YY11604 CA21 AD001 AD015 CA00 CA30 YY31704 AD116 CW01 AB317 TT0200 CA11 AD317 TT2401 CO0200 TT2312 CX2401 TT0213 OQ020 CO0213 OQ240 CO2312 OQ021 TT3414 CO3414 OQ231 OQ341
 """.split()
 
 
@@ -40,7 +39,10 @@ def tile_exchange_correlation_block_k4_kernel(
         banks = [psum.tile([P, W], F32, name="bank%d" % b) for b in range(8)]
         p_raw = [sb("p_raw%d" % G, [P, 2, W], I32) for G in range(4)]
         p_perm = [sb("p_perm%d" % G, [P, 4, 2, P], I32) for G in range(4)]
-        ps_raw = sb("ps_raw", [P, 2, R // 4], I32)
+        ps_raw = [sb("ps_raw%d" % n, [P, 2, R // 8], I32) for n in range(2)]
+        warm_in = sb("warm_in", [P, W], BF16)
+        warm_codes = sb("warm_codes", [P, P], I32)
+        warm_scales = sb("warm_scales", [P, P], U8)
         ps_perm = sb("ps_perm", [P, 4, 2, R // 16], I32)
         ca_words = sb("ca_words", [P, 2, 2 * NA], U8)
         ca_scales = sb("ca_scales", [P, 2, NA], U8)
@@ -56,22 +58,18 @@ def tile_exchange_correlation_block_k4_kernel(
         units = [(c, G) for c in range(3) for G in range(4)]
         rows = {u: sb("rows%d%d" % u, [P, 4, W], BF16) for u in units}
         grp_ring = [sb("grp%d" % n, [P, W, 4], BF16) for n in range(4)]
-        turns = [s for s in ORDER if s[0] == "I"]
-        grp = {(int(s[2]), int(s[3])): grp_ring[n % 4] for n, s in enumerate(turns)}
+        turns = []
+        for s in ORDER:
+            if s[0] == "I" and s[2:4] not in turns:
+                turns.append(s[2:4])
+        grp = {(int(s[0]), int(s[1])): grp_ring[n % 4] for n, s in enumerate(turns)}
         codes = {u: sb("codes%d%d" % u, [P, W], I32) for u in units}
         scales = {u: sb("scales%d%d" % u, [P, W], U8) for u in units}
         y_sb = {(i, h): sb("y%d%d" % (i, h), [P, W], F32) for i in range(4) for h in range(2)}
         y_bf = {(i, h): sb("ybf%d%d" % (i, h), [P, W], BF16) for i in range(4) for h in range(2)}
         o_grp = [sb("o_grp%d" % h, [P, W, 4], BF16) for h in range(2)]
         o_codes = [sb("o_codes%d" % h, [P, W], I32) for h in range(2)]
-        o_scales = [sb("o_scales%d" % h, [P, W], U8) for h in range(2)]
-
-        nc.vector.memset(ps_raw[:], 0)
-        nc.vector.memset(ca_scales[:].rearrange("p g n -> p (g n)").bitcast(I32), 0)
-        nc.gpsimd.dma_start(out=fac_raw[0:4, :], in_=quad.rearrange("(G n) -> G n", G=4))
-        nc.gpsimd.dma_start(out=fac_raw[4:8, :], in_=vxc.rearrange("(G n) -> G n", G=4))
-        nc.gpsimd.memset(fac_rows[:], 0.0)
-        make_identity(nc, ident[:])
+        o_scales = sb("o_scales", [P, 2, W], U8)
 
         pw = prim_words.rearrange("g p n t -> p g (n t)").bitcast(I32)
         psc = prim_scales.rearrange("g q n -> q g n").bitcast(I32)
@@ -80,21 +78,36 @@ def tile_exchange_correlation_block_k4_kernel(
         def load_p(G):
             nc.sync.dma_start(out=p_raw[G][:], in_=pw[:, :, G * W : (G + 1) * W])
 
+        def load_ps(n, Q0, Q1):
+            for Q in range(Q0, Q1):
+                nc.sync.dma_start(
+                    out=ps_raw[n][32 * Q : 32 * Q + 4, :, :], in_=psc[4 * Q : 4 * Q + 4, :, 256 * n : 256 * (n + 1)]
+                )
+
         def load_cb(h, g):
             src = coef_b[g * W : (g + 1) * W, h * W : (h + 1) * W]
             nc.sync.dma_start(out=cb_raw[h, g][:], in_=src.rearrange("(p j) n -> p j n", j=4))
 
+        nc.vector.memset(warm_in[:], 0.0)
+        nc.vector.memset(ps_raw[0][:], 0)
+        nc.vector.quantize_mx(out=warm_codes[:].bitcast(FP8X4), scales=warm_scales[:], in_=warm_in[:])
+        nc.vector.memset(ca_scales[:].rearrange("p g n -> p (g n)").bitcast(I32), 0)
+        nc.vector.memset(fac_rows[:], 0.0)
+        nc.vector.memset(ps_raw[1][:], 0)
+        make_identity(nc, ident[:])
+
+        nc.sync.dma_start(out=fac_raw[0:4, :], in_=quad.rearrange("(G n) -> G n", G=4))
+        nc.sync.dma_start(out=fac_raw[4:8, :], in_=vxc.rearrange("(G n) -> G n", G=4))
+        load_ps(0, 0, 2)
         nc.sync.dma_start(out=ca_words[:].bitcast(I32), in_=coef_a_words.rearrange("g p n -> p g n").bitcast(I32))
         load_p(0)
+        load_ps(0, 2, 4)
         for Q in range(4):
-            nc.sync.dma_start(out=ps_raw[32 * Q : 32 * Q + 4, :, :], in_=psc[4 * Q : 4 * Q + 4, :, :])
-        for Q in range(4):
-            nc.sync.dma_start(
-                out=ca_scales[32 * Q : 32 * Q + 4, :, :].bitcast(I32), in_=cas[4 * Q : 4 * Q + 4, :, :]
-            )
-        load_p(1)
+            nc.sync.dma_start(out=ca_scales[32 * Q : 32 * Q + 4, :, :].bitcast(I32), in_=cas[4 * Q : 4 * Q + 4, :, :])
         load_cb(0, 0)
+        load_p(1)
         load_cb(0, 1)
+        load_ps(1, 0, 4)
         load_p(2)
         load_p(3)
         load_cb(1, 0)
@@ -103,14 +116,29 @@ def tile_exchange_correlation_block_k4_kernel(
             src = h_rest[:, h * W : (h + 1) * W]
             nc.sync.dma_start(out=h_sb[h][:], in_=src.rearrange("(a p) j -> p a j", p=P))
 
+        def warm_up(count):
+            for n in range(count):
+                nc.tensor.matmul_mx(
+                    out=banks[7][:, 0:P],
+                    lhsT=warm_codes[:].bitcast(FP8X4),
+                    lhsT_scale=warm_scales[:],
+                    rhs=warm_codes[:].bitcast(FP8X4),
+                    rhs_scale=warm_scales[:],
+                    start=True,
+                    stop=True,
+                )
+
+        warm_up(WARM[0])
+
         nc.scalar.activation(
             out=fac_rows[0:8, :].rearrange("v (t q e) -> v t q e", t=4, e=8),
             in_=fac_raw[:].rearrange("v (q t e) -> v t q e", t=4, e=8),
             func=COPY,
         )
         for t in range(4):
-            nc.tensor.transpose(banks[7][:, t * P : (t + 1) * P], fac_rows[:, t * P : (t + 1) * P], ident[:])
-        nc.scalar.activation(out=fac[:], in_=banks[7][:].rearrange("p (t v) -> p t v", t=4)[:, :, 0:8], func=COPY)
+            nc.tensor.transpose(banks[6][:, t * P : (t + 1) * P], fac_rows[:, t * P : (t + 1) * P], ident[:])
+        warm_up(WARM[1])
+        nc.scalar.activation(out=fac[:], in_=banks[6][:].rearrange("p (t v) -> p t v", t=4)[:, :, 0:8], func=COPY)
 
         def permute_words(G):
             nc.vector.tensor_copy(
@@ -122,12 +150,13 @@ def tile_exchange_correlation_block_k4_kernel(
             for g in range(2):
                 nc.vector.tensor_copy(
                     out=ps_perm[:, :, g, 32 * G0 : 32 * G1].rearrange("p t (b e) -> p t b e", e=2),
-                    in_=ps_raw[:, g, P * G0 : P * G1].rearrange("p (b t e) -> p t b e", t=4, e=2),
+                    in_=ps_raw[G0 // 2][:, g, P * (G0 % 2) : P * (G1 - G0 + G0 % 2)].rearrange("p (b t e) -> p t b e", t=4, e=2),
                 )
 
-        def interleave(engine, dst, src):
-            out = dst[:].rearrange("p (c i) t -> p c t i", i=4)
-            in_ = src[:].rearrange("p t (c i) -> p c t i", i=4)
+        def interleave(engine, dst, src, part):
+            cols = slice(0, W) if part == 2 else slice(part * W // 2, (part + 1) * W // 2)
+            out = dst[:, cols, :].rearrange("p (c i) t -> p c t i", i=4)
+            in_ = src[:, :, cols].rearrange("p t (c i) -> p c t i", i=4)
             if engine == "V":
                 nc.vector.tensor_copy(out=out, in_=in_)
             else:
@@ -140,9 +169,9 @@ def tile_exchange_correlation_block_k4_kernel(
                 in_=src[:, c0:c1, :].rearrange("p w j -> p (w j)"),
             )
 
-        def stage1(c, G, b0):
+        def stage1(c, G, bs):
             for t in range(4):
-                bank = banks[(b0 + t) % 8]
+                bank = banks[bs[t]]
                 for g in range(2):
                     if c == 0:
                         rhs = ca_words[:, g, :].bitcast(FP4X4)
@@ -186,8 +215,8 @@ def tile_exchange_correlation_block_k4_kernel(
                 op=ADD,
             )
 
-        def cast(i, h):
-            nc.scalar.copy(
+        def cast(i, h, copy):
+            copy(
                 out=y_bf[i, h][:].rearrange("p (u m e) -> p u m e", u=2, e=2),
                 in_=y_sb[i, h][:].rearrange("p (m u e) -> p u m e", u=2, e=2),
             )
@@ -199,23 +228,27 @@ def tile_exchange_correlation_block_k4_kernel(
                     s = 2 * (i - i0) + u
                     nc.tensor.transpose(banks[b][:, s * P : (s + 1) * P], words[:, u * P : (u + 1) * P], ident[:])
 
-        def copy_out(i0, i1, h, b):
+        def copy_out(i0, i1, h, b, copy):
             n = i1 - i0
             dst = o_grp[h][:, i0 * P : i1 * P, :].rearrange("p m t -> p (m t)").bitcast(F32)
-            nc.scalar.copy(
+            copy(
                 out=dst.rearrange("p (a m u) -> p a m u", a=n, u=2),
                 in_=banks[b][:, 0 : 2 * n * P].rearrange("p (a u m) -> p a m u", a=n, u=2),
             )
 
         def out_quant(i0, i1, h):
-            quantize(o_codes[h], o_scales[h], o_grp[h], i0 * P, i1 * P)
+            quantize(o_codes[h], o_scales[:, h, :], o_grp[h], i0 * P, i1 * P)
+            if i1 < 3:
+                return
+            m0 = 3 * P if (h, i1) == (1, 4) else 0
             dst = out_1[h].rearrange("p m t -> p (m t)").bitcast(I32)
-            nc.sync.dma_start(out=dst[:, i0 * P : i1 * P], in_=o_codes[h][:, i0 * P : i1 * P])
-            if i1 == 4:
+            nc.sync.dma_start(out=dst[:, m0 : i1 * P], in_=o_codes[h][:, m0 : i1 * P])
+            if (h, i1) == (1, 4):
+                rows_out = out_2.rearrange("g q m -> q g m").bitcast(I32)
                 for Q in range(4):
-                    nc.sync.dma_start(
-                        out=out_2[h, 4 * Q : 4 * Q + 4, :].bitcast(I32),
-                        in_=o_scales[h][32 * Q : 32 * Q + 4, :].bitcast(I32),
+                    queue = nc.scalar if Q < 2 else nc.sync
+                    queue.dma_start(
+                        out=rows_out[4 * Q : 4 * Q + 4, :, :], in_=o_scales[32 * Q : 32 * Q + 4, :, :].bitcast(I32)
                     )
 
         for step in ORDER:
@@ -226,17 +259,17 @@ def tile_exchange_correlation_block_k4_kernel(
             elif kind == "SP":
                 permute_scales(a[0], a[1])
             elif kind == "CV":
-                interleave("V", cb_grp[a[0], a[1]], cb_raw[a[0], a[1]])
+                interleave("V", cb_grp[a[0], a[1]], cb_raw[a[0], a[1]], a[2])
             elif kind == "CS":
-                interleave("S", cb_grp[a[0], a[1]], cb_raw[a[0], a[1]])
+                interleave("S", cb_grp[a[0], a[1]], cb_raw[a[0], a[1]], a[2])
             elif kind == "CQ":
                 quantize(cb_codes[a[0], a[1]], cb_scales[a[0], a[1]], cb_grp[a[0], a[1]], 0, W)
             elif kind == "UU":
-                stage1(a[0], a[1], a[2])
+                stage1(a[0], a[1], a[2:6])
             elif kind == "IV":
-                interleave("V", grp[a[0], a[1]], rows[a[0], a[1]])
+                interleave("V", grp[a[0], a[1]], rows[a[0], a[1]], a[2])
             elif kind == "IS":
-                interleave("S", grp[a[0], a[1]], rows[a[0], a[1]])
+                interleave("S", grp[a[0], a[1]], rows[a[0], a[1]], a[2])
             elif kind == "QQ":
                 quantize(codes[a[0], a[1]], scales[a[0], a[1]], grp[a[0], a[1]], 0, W)
             elif kind == "YY":
@@ -246,10 +279,14 @@ def tile_exchange_correlation_block_k4_kernel(
             elif kind == "AB":
                 add_round(a[0], a[1], a[2])
             elif kind == "CA":
-                cast(a[0], a[1])
+                cast(a[0], a[1], nc.scalar.copy)
+            elif kind == "CW":
+                cast(a[0], a[1], nc.vector.tensor_copy)
             elif kind == "TT":
                 turn(a[0], a[1], a[2], a[3])
             elif kind == "CO":
-                copy_out(a[0], a[1], a[2], a[3])
+                copy_out(a[0], a[1], a[2], a[3], nc.scalar.copy)
+            elif kind == "CX":
+                copy_out(a[0], a[1], a[2], a[3], nc.vector.tensor_copy)
             else:
                 out_quant(a[0], a[1], a[2])

@@ -17,11 +17,16 @@ ADD = mybir.AluOpType.add
 
 P = 128
 W = 512
-WARM = (14, 8)
-
-ORDER = """
-PP0 SP02 CS000 CV001 PP1 UU000123 CQ00 CV012 CQ01 PP2 SP24 PP3 CV102 CV112 UU014567 IV012 IV002 UU110123 CQ10 UU034567 QQ00 UU100123 UU124567 UU020123 IV032 IV112 QQ01 UU134567 QQ03 CQ11 IV122 UU210123 IV022 UU204567 QQ11 UU230123 QQ12 IV132 IV102 QQ02 QQ10 IV202 QQ13 UU224567 IV212 QQ20 YY10004 IV222 YY00104 QQ21 IS232 QQ22 QQ23 YY20204 YY30304 AD100 YY21404 AD202 CA20 AD303 CA10 YY01504 AD214 YY11604 CA21 AD001 AD015 CA00 CA30 YY31704 AD116 CW01 AB317 TT0200 CA11 AD317 TT2401 CO0200 TT2312 CX2401 TT0213 OQ020 CO0213 OQ240 CO2312 OQ021 TT3414 CO3414 OQ231 OQ341
-""".split()
+PACK = 4
+CHUNKS = R // W
+GROUPS = K // W
+HALVES = NB // W
+ROW_TILES = NA // P
+BANKS = 8
+SET_A, SET_B0, SET_B1 = 0, 1, 2
+ROW_BUFS = 10
+PAIR_BUFS = 3
+WARM_BEFORE, WARM_AFTER = 14, 21
 
 
 def tile_exchange_correlation_block_k4_kernel(
@@ -36,257 +41,334 @@ def tile_exchange_correlation_block_k4_kernel(
         def sb(name, shape, dtype):
             return keep.tile(shape, dtype, name=name, align_bytes=64)
 
-        banks = [psum.tile([P, W], F32, name="bank%d" % b) for b in range(8)]
-        p_raw = [sb("p_raw%d" % G, [P, 2, W], I32) for G in range(4)]
-        p_perm = [sb("p_perm%d" % G, [P, 4, 2, P], I32) for G in range(4)]
-        ps_raw = [sb("ps_raw%d" % n, [P, 2, R // 8], I32) for n in range(2)]
-        warm_in = sb("warm_in", [P, W], BF16)
-        warm_codes = sb("warm_codes", [P, P], I32)
-        warm_scales = sb("warm_scales", [P, P], U8)
-        ps_perm = sb("ps_perm", [P, 4, 2, R // 16], I32)
-        ca_words = sb("ca_words", [P, 2, 2 * NA], U8)
-        ca_scales = sb("ca_scales", [P, 2, NA], U8)
-        cb_raw = {(h, g): sb("cb_raw%d%d" % (h, g), [P, 4, W], BF16) for h in range(2) for g in range(2)}
-        cb_grp = {(h, g): sb("cb_grp%d%d" % (h, g), [P, W, 4], BF16) for h in range(2) for g in range(2)}
-        cb_codes = {(h, g): sb("cb_codes%d%d" % (h, g), [P, W], I32) for h in range(2) for g in range(2)}
-        cb_scales = {(h, g): sb("cb_scales%d%d" % (h, g), [P, W], U8) for h in range(2) for g in range(2)}
-        h_sb = [sb("h_sb%d" % h, [P, 4, W], BF16) for h in range(2)]
-        fac_raw = sb("fac_raw", [8, W], BF16)
-        fac_rows = sb("fac_rows", [P, W], F32)
-        fac = sb("fac", [P, 4, 8], F32)
+        banks = [psum.tile([P, W], F32, name="bank%d" % b) for b in range(BANKS)]
+        banks_taken = []
+
+        def take_bank():
+            banks_taken.append(1)
+            return banks[(len(banks_taken) - 1) % BANKS]
+
+        p_raw = [sb("p_raw%d" % c, [P, GROUPS, W], I32) for c in range(CHUNKS)]
+        p_words = [sb("p_words%d" % c, [P, PACK, GROUPS, P], I32) for c in range(CHUNKS)]
+        ps_raw = [sb("ps_raw%d" % part, [P, GROUPS, 2 * W // 4], I32) for part in range(2)]
+        p_scales = [sb("p_scales%d" % part, [P, PACK, GROUPS, 2 * P // 4], I32) for part in range(2)]
+        ca_words = sb("ca_words", [P, GROUPS, 2 * NA], U8)
+        ca_scales = sb("ca_scales", [P, GROUPS, NA], U8)
+        cb_raw = {(h, g): sb("cb_raw%d%d" % (h, g), [P, PACK, W], BF16) for h in range(HALVES) for g in range(GROUPS)}
+        cb_mixed = [sb("cb_mixed%d" % h, [P, GROUPS * W, PACK], BF16) for h in range(HALVES)]
+        cb_words = [sb("cb_words%d" % h, [P, GROUPS * W], I32) for h in range(HALVES)]
+        cb_scales = [sb("cb_scales%d" % h, [P, GROUPS * W], U8) for h in range(HALVES)]
+        rest = [sb("rest%d" % h, [P, ROW_TILES, W], BF16) for h in range(HALVES)]
+        factor_raw = sb("factor_raw", [2 * CHUNKS, W], BF16)
+        factor_rows = sb("factor_rows", [P, W], F32)
+        factor = sb("factor", [P, 2 * CHUNKS, PACK], F32)
         ident = sb("ident", [P, P], F32)
-        units = [(c, G) for c in range(3) for G in range(4)]
-        rows = {u: sb("rows%d%d" % u, [P, 4, W], BF16) for u in units}
-        grp_ring = [sb("grp%d" % n, [P, W, 4], BF16) for n in range(4)]
-        turns = []
-        for s in ORDER:
-            if s[0] == "I" and s[2:4] not in turns:
-                turns.append(s[2:4])
-        grp = {(int(s[0]), int(s[1])): grp_ring[n % 4] for n, s in enumerate(turns)}
-        codes = {u: sb("codes%d%d" % u, [P, W], I32) for u in units}
-        scales = {u: sb("scales%d%d" % u, [P, W], U8) for u in units}
-        y_sb = {(i, h): sb("y%d%d" % (i, h), [P, W], F32) for i in range(4) for h in range(2)}
-        y_bf = {(i, h): sb("ybf%d%d" % (i, h), [P, W], BF16) for i in range(4) for h in range(2)}
-        o_grp = [sb("o_grp%d" % h, [P, W, 4], BF16) for h in range(2)]
-        o_codes = [sb("o_codes%d" % h, [P, W], I32) for h in range(2)]
-        o_scales = sb("o_scales", [P, 2, W], U8)
+        warm_in = sb("warm_in", [P, W], BF16)
+        warm_words = sb("warm_words", [P, P], I32)
+        warm_scales = sb("warm_scales", [P, P], U8)
+        unit_rows = [sb("unit_rows%d" % n, [P, PACK, W], BF16) for n in range(ROW_BUFS)]
+        pair_mixed = [sb("pair_mixed%d" % n, [P, 2 * W, PACK], BF16) for n in range(PAIR_BUFS)]
+        pair_words = [sb("pair_words%d" % n, [P, 2 * W], I32) for n in range(3 * CHUNKS // 2)]
+        pair_scales = [sb("pair_scales%d" % n, [P, 2 * W], U8) for n in range(3 * CHUNKS // 2)]
+        tiles = [(i, h) for h in range(HALVES) for i in range(ROW_TILES)]
+        y_f32 = {ih: sb("y_f32_%d%d" % ih, [P, W], F32) for ih in tiles}
+        y_bf16 = {ih: sb("y_bf16_%d%d" % ih, [P, W], BF16) for ih in tiles}
+        out_mixed = [sb("out_mixed%d" % h, [P, NA, PACK], BF16) for h in range(HALVES)]
+        out_words = [sb("out_words%d" % h, [P, NA], I32) for h in range(HALVES)]
+        out_scales = sb("out_scales", [P, HALVES, NA], U8)
 
-        pw = prim_words.rearrange("g p n t -> p g (n t)").bitcast(I32)
-        psc = prim_scales.rearrange("g q n -> q g n").bitcast(I32)
-        cas = coef_a_scales.rearrange("g q n -> q g n").bitcast(I32)
+        nc.gpsimd.memset(ps_raw[0][:], 0)
+        make_identity(nc, ident[:])
+        nc.vector.memset(warm_in[:], 0.0)
+        nc.vector.memset(ca_scales[:].rearrange("p g n -> p (g n)").bitcast(I32), 0)
+        nc.vector.quantize_mx(out=warm_words[:].bitcast(FP8X4), scales=warm_scales[:], in_=warm_in[:])
+        nc.vector.memset(factor_rows[:], 0.0)
+        nc.vector.memset(ps_raw[1][:], 0)
 
-        def load_p(G):
-            nc.sync.dma_start(out=p_raw[G][:], in_=pw[:, :, G * W : (G + 1) * W])
+        prim_words_hbm = prim_words.rearrange("g p n t -> p g (n t)").bitcast(I32)
+        prim_scales_hbm = prim_scales.rearrange("g q n -> q g n").bitcast(I32)
+        ca_scales_hbm = coef_a_scales.rearrange("g q n -> q g n").bitcast(I32)
 
-        def load_ps(n, Q0, Q1):
-            for Q in range(Q0, Q1):
+        def load_p(chunk):
+            nc.sync.dma_start(out=p_raw[chunk][:], in_=prim_words_hbm[:, :, chunk * W : (chunk + 1) * W])
+
+        def load_p_scales(part, quadrants):
+            cols = slice(part * 2 * W // 4, (part + 1) * 2 * W // 4)
+            for Q in quadrants:
                 nc.sync.dma_start(
-                    out=ps_raw[n][32 * Q : 32 * Q + 4, :, :], in_=psc[4 * Q : 4 * Q + 4, :, 256 * n : 256 * (n + 1)]
+                    out=ps_raw[part][32 * Q : 32 * Q + 4, :, :], in_=prim_scales_hbm[4 * Q : 4 * Q + 4, :, cols]
                 )
 
         def load_cb(h, g):
             src = coef_b[g * W : (g + 1) * W, h * W : (h + 1) * W]
-            nc.sync.dma_start(out=cb_raw[h, g][:], in_=src.rearrange("(p j) n -> p j n", j=4))
+            nc.sync.dma_start(out=cb_raw[h, g][:], in_=src.rearrange("(p t) n -> p t n", t=PACK))
 
-        nc.vector.memset(warm_in[:], 0.0)
-        nc.vector.memset(ps_raw[0][:], 0)
-        nc.vector.quantize_mx(out=warm_codes[:].bitcast(FP8X4), scales=warm_scales[:], in_=warm_in[:])
-        nc.vector.memset(ca_scales[:].rearrange("p g n -> p (g n)").bitcast(I32), 0)
-        nc.vector.memset(fac_rows[:], 0.0)
-        nc.vector.memset(ps_raw[1][:], 0)
-        make_identity(nc, ident[:])
-
-        nc.sync.dma_start(out=fac_raw[0:4, :], in_=quad.rearrange("(G n) -> G n", G=4))
-        nc.sync.dma_start(out=fac_raw[4:8, :], in_=vxc.rearrange("(G n) -> G n", G=4))
-        load_ps(0, 0, 2)
+        nc.sync.dma_start(out=factor_raw[0:CHUNKS, :], in_=quad.rearrange("(c n) -> c n", c=CHUNKS))
+        nc.sync.dma_start(out=factor_raw[CHUNKS : 2 * CHUNKS, :], in_=vxc.rearrange("(c n) -> c n", c=CHUNKS))
+        load_p_scales(0, (0, 1))
         nc.sync.dma_start(out=ca_words[:].bitcast(I32), in_=coef_a_words.rearrange("g p n -> p g n").bitcast(I32))
         load_p(0)
-        load_ps(0, 2, 4)
+        load_p_scales(0, (2, 3))
         for Q in range(4):
-            nc.sync.dma_start(out=ca_scales[32 * Q : 32 * Q + 4, :, :].bitcast(I32), in_=cas[4 * Q : 4 * Q + 4, :, :])
+            nc.sync.dma_start(
+                out=ca_scales[32 * Q : 32 * Q + 4, :, :].bitcast(I32), in_=ca_scales_hbm[4 * Q : 4 * Q + 4, :, :]
+            )
         load_cb(0, 0)
         load_p(1)
         load_cb(0, 1)
-        load_ps(1, 0, 4)
+        load_p_scales(1, (0, 1, 2, 3))
         load_p(2)
         load_p(3)
         load_cb(1, 0)
         load_cb(1, 1)
-        for h in range(2):
+        for h in range(HALVES):
             src = h_rest[:, h * W : (h + 1) * W]
-            nc.sync.dma_start(out=h_sb[h][:], in_=src.rearrange("(a p) j -> p a j", p=P))
+            nc.sync.dma_start(out=rest[h][:], in_=src.rearrange("(i p) j -> p i j", p=P))
 
         def warm_up(count):
             for n in range(count):
                 nc.tensor.matmul_mx(
                     out=banks[7][:, 0:P],
-                    lhsT=warm_codes[:].bitcast(FP8X4),
+                    lhsT=warm_words[:].bitcast(FP8X4),
                     lhsT_scale=warm_scales[:],
-                    rhs=warm_codes[:].bitcast(FP8X4),
+                    rhs=warm_words[:].bitcast(FP8X4),
                     rhs_scale=warm_scales[:],
                     start=True,
                     stop=True,
                 )
 
-        warm_up(WARM[0])
-
+        warm_up(WARM_BEFORE)
         nc.scalar.activation(
-            out=fac_rows[0:8, :].rearrange("v (t q e) -> v t q e", t=4, e=8),
-            in_=fac_raw[:].rearrange("v (q t e) -> v t q e", t=4, e=8),
+            out=factor_rows[0 : 2 * CHUNKS, :].rearrange("v (t q e) -> v t q e", t=PACK, e=8),
+            in_=factor_raw[:].rearrange("v (q t e) -> v t q e", t=PACK, e=8),
             func=COPY,
         )
-        for t in range(4):
-            nc.tensor.transpose(banks[6][:, t * P : (t + 1) * P], fac_rows[:, t * P : (t + 1) * P], ident[:])
-        warm_up(WARM[1])
-        nc.scalar.activation(out=fac[:], in_=banks[6][:].rearrange("p (t v) -> p t v", t=4)[:, :, 0:8], func=COPY)
+        for t in range(PACK):
+            nc.tensor.transpose(banks[6][:, t * P : (t + 1) * P], factor_rows[:, t * P : (t + 1) * P], ident[:])
+        warm_up(WARM_AFTER)
+        nc.scalar.activation(
+            out=factor[:].rearrange("p v t -> p t v"),
+            in_=banks[6][:].rearrange("p (t v) -> p t v", t=PACK)[:, :, 0 : 2 * CHUNKS],
+            func=COPY,
+        )
 
-        def permute_words(G):
+        def reorder_words(chunk):
             nc.vector.tensor_copy(
-                out=p_perm[G][:].rearrange("p t g (q e) -> p t (g q) e", e=8),
-                in_=p_raw[G][:].rearrange("p g (q t e) -> p t (g q) e", t=4, e=8),
+                out=p_words[chunk][:].rearrange("p t g (q e) -> p t (g q) e", e=8),
+                in_=p_raw[chunk][:].rearrange("p g (q t e) -> p t (g q) e", t=PACK, e=8),
             )
 
-        def permute_scales(G0, G1):
-            for g in range(2):
-                nc.vector.tensor_copy(
-                    out=ps_perm[:, :, g, 32 * G0 : 32 * G1].rearrange("p t (b e) -> p t b e", e=2),
-                    in_=ps_raw[G0 // 2][:, g, P * (G0 % 2) : P * (G1 - G0 + G0 % 2)].rearrange("p (b t e) -> p t b e", t=4, e=2),
-                )
-
-        def interleave(engine, dst, src, part):
-            cols = slice(0, W) if part == 2 else slice(part * W // 2, (part + 1) * W // 2)
-            out = dst[:, cols, :].rearrange("p (c i) t -> p c t i", i=4)
-            in_ = src[:, :, cols].rearrange("p t (c i) -> p c t i", i=4)
-            if engine == "V":
-                nc.vector.tensor_copy(out=out, in_=in_)
-            else:
-                nc.scalar.copy(out=out, in_=in_)
-
-        def quantize(dst, sc, src, c0, c1):
-            nc.vector.quantize_mx(
-                out=dst[:, c0:c1].bitcast(FP8X4),
-                scales=sc[:, c0:c1],
-                in_=src[:, c0:c1, :].rearrange("p w j -> p (w j)"),
+        def reorder_scales(part):
+            nc.vector.tensor_copy(
+                out=p_scales[part][:].rearrange("p t g (b e) -> p t (g b) e", e=2),
+                in_=ps_raw[part][:].rearrange("p g (b t e) -> p t (g b) e", t=PACK, e=2),
             )
 
-        def stage1(c, G, bs):
-            for t in range(4):
-                bank = banks[bs[t]]
-                for g in range(2):
-                    if c == 0:
-                        rhs = ca_words[:, g, :].bitcast(FP4X4)
-                        rhs_scale = ca_scales[:, g, :]
-                    else:
-                        rhs = cb_codes[c - 1, g][:].bitcast(FP8X4)
-                        rhs_scale = cb_scales[c - 1, g][:]
-                    nc.tensor.matmul_mx(
-                        out=bank[:],
-                        lhsT=p_perm[G][:, t, g, :].bitcast(FP8X4),
-                        lhsT_scale=ps_perm[:, t, g, 32 * G : 32 * (G + 1)].bitcast(U8),
-                        rhs=rhs,
-                        rhs_scale=rhs_scale,
-                        start=(g == 0),
-                        stop=(g == 1),
-                    )
-                v = G if c == 0 else 4 + G
-                nc.scalar.activation(out=rows[c, G][:, t, :], in_=bank[:], func=COPY, scale=fac[:, t, v : v + 1])
+        def interleave(copy, mixed, rows):
+            copy(
+                out=mixed.rearrange("p (c i) t -> p c t i", i=4),
+                in_=rows.rearrange("p t (c i) -> p c t i", i=4),
+            )
 
-        def stage2(i, h, b, G0, G1):
-            for G in range(G0, G1):
+        def quantize(words, scales, mixed):
+            nc.vector.quantize_mx(out=words.bitcast(FP8X4), scales=scales, in_=mixed.rearrange("p w t -> p (w t)"))
+
+        def interleave_cb(copy, h, g, c0, c1):
+            interleave(copy, cb_mixed[h][:, g * W + c0 : g * W + c1, :], cb_raw[h, g][:, :, c0:c1])
+
+        def quantize_cb(h, g0, g1):
+            cols = slice(g0 * W, g1 * W)
+            quantize(cb_words[h][:, cols], cb_scales[h][:, cols], cb_mixed[h][:, cols, :])
+
+        def unit_place(panel, chunk):
+            n = CHUNKS * panel + chunk
+            return n // 2, slice(n % 2 * W, (n % 2 + 1) * W)
+
+        def build(panel, chunk, passes):
+            rows = unit_rows[(CHUNKS * panel + chunk) % ROW_BUFS]
+            v = chunk if panel == SET_A else CHUNKS + chunk
+            slot_banks = [take_bank() for t in range(PACK)]
+            for t, g in passes:
+                if panel == SET_A:
+                    rhs, rhs_scale = ca_words[:, g, :].bitcast(FP4X4), ca_scales[:, g, :]
+                else:
+                    cols = slice(g * W, (g + 1) * W)
+                    rhs, rhs_scale = cb_words[panel - 1][:, cols].bitcast(FP8X4), cb_scales[panel - 1][:, cols]
                 nc.tensor.matmul_mx(
-                    out=banks[b][:],
-                    lhsT=codes[0, G][:, i * P : (i + 1) * P].bitcast(FP8X4),
-                    lhsT_scale=scales[0, G][:, i * P : (i + 1) * P],
-                    rhs=codes[1 + h, G][:].bitcast(FP8X4),
-                    rhs_scale=scales[1 + h, G][:],
-                    start=(G == 0),
-                    stop=(G == 3),
+                    out=slot_banks[t][:],
+                    lhsT=p_words[chunk][:, t, g, :].bitcast(FP8X4),
+                    lhsT_scale=p_scales[chunk // 2][:, t, g, 32 * (chunk % 2) : 32 * (chunk % 2 + 1)].bitcast(U8),
+                    rhs=rhs,
+                    rhs_scale=rhs_scale,
+                    start=(g == 0),
+                    stop=(g == GROUPS - 1),
                 )
+                if g == GROUPS - 1:
+                    nc.scalar.activation(
+                        out=rows[:, t, :], in_=slot_banks[t][:], func=COPY, scale=factor[:, v, t : t + 1]
+                    )
 
-        def add_rest(i, h, b):
-            nc.vector.tensor_tensor(out=y_sb[i, h][:], in0=banks[b][:], in1=h_sb[h][:, i, :], op=ADD)
-            nc.sync.dma_start(out=out_0[i * P : (i + 1) * P, h * W : (h + 1) * W], in_=y_sb[i, h][:])
+        bank_by_bank = [(t, g) for t in range(PACK) for g in range(GROUPS)]
+        group_by_group = [(t, g) for g in range(GROUPS) for t in range(PACK)]
 
-        def add_round(i, h, b):
+        def interleave_unit(copy, panel, chunk):
+            pair, cols = unit_place(panel, chunk)
+            rows = unit_rows[(CHUNKS * panel + chunk) % ROW_BUFS]
+            interleave(copy, pair_mixed[pair % PAIR_BUFS][:, cols, :], rows[:])
+
+        def quantize_unit(panel, chunk):
+            pair, cols = unit_place(panel, chunk)
+            quantize(pair_words[pair][:, cols], pair_scales[pair][:, cols], pair_mixed[pair % PAIR_BUFS][:, cols, :])
+
+        def quantize_pair(pair):
+            quantize(pair_words[pair][:], pair_scales[pair][:], pair_mixed[pair % PAIR_BUFS][:])
+
+        def contract(i, h, c0, c1):
+            acc = take_bank()[:, 0 : c1 - c0]
+            for chunk in range(CHUNKS):
+                a_pair, a_cols = unit_place(SET_A, chunk)
+                b_pair, b_cols = unit_place(SET_B0 + h, chunk)
+                a_cols = slice(a_cols.start + i * P, a_cols.start + (i + 1) * P)
+                b_cols = slice(b_cols.start + c0, b_cols.start + c1)
+                nc.tensor.matmul_mx(
+                    out=acc,
+                    lhsT=pair_words[a_pair][:, a_cols].bitcast(FP8X4),
+                    lhsT_scale=pair_scales[a_pair][:, a_cols],
+                    rhs=pair_words[b_pair][:, b_cols].bitcast(FP8X4),
+                    rhs_scale=pair_scales[b_pair][:, b_cols],
+                    start=(chunk == 0),
+                    stop=(chunk == CHUNKS - 1),
+                )
+            return acc
+
+        def add_rest(i, h, acc, c0, c1):
+            nc.vector.tensor_tensor(out=y_f32[i, h][:, c0:c1], in0=acc, in1=rest[h][:, i, c0:c1], op=ADD)
+
+        def store_y(i, h):
+            nc.sync.dma_start(out=out_0[i * P : (i + 1) * P, h * W : (h + 1) * W], in_=y_f32[i, h][:])
+
+        def round_y(copy, i, h):
+            copy(
+                out=y_bf16[i, h][:].rearrange("p (u m e) -> p u m e", u=2, e=2),
+                in_=y_f32[i, h][:].rearrange("p (m u e) -> p u m e", u=2, e=2),
+            )
+
+        def add_rest_rounded(i, h, acc, c0, c1):
             nc.vector.tensor_tensor(
-                out=y_bf[i, h][:].rearrange("p (u m e) -> p u m e", u=2, e=2),
-                in0=banks[b][:].rearrange("p (m u e) -> p u m e", u=2, e=2),
-                in1=h_sb[h][:, i, :].rearrange("p (m u e) -> p u m e", u=2, e=2),
+                out=y_bf16[i, h][:].rearrange("p (u m e) -> p u m e", u=2, e=2)[:, :, c0 // PACK : c1 // PACK, :],
+                in0=acc.rearrange("p (m u e) -> p u m e", u=2, e=2),
+                in1=rest[h][:, i, c0:c1].rearrange("p (m u e) -> p u m e", u=2, e=2),
                 op=ADD,
             )
 
-        def cast(i, h, copy):
-            copy(
-                out=y_bf[i, h][:].rearrange("p (u m e) -> p u m e", u=2, e=2),
-                in_=y_sb[i, h][:].rearrange("p (m u e) -> p u m e", u=2, e=2),
-            )
-
-        def turn(i0, i1, h, b):
+        def turn(i0, i1, h):
+            bank = take_bank()
             for i in range(i0, i1):
-                words = y_bf[i, h][:].bitcast(F32)
+                words = y_bf16[i, h][:].bitcast(F32)
                 for u in range(2):
                     s = 2 * (i - i0) + u
-                    nc.tensor.transpose(banks[b][:, s * P : (s + 1) * P], words[:, u * P : (u + 1) * P], ident[:])
+                    nc.tensor.transpose(bank[:, s * P : (s + 1) * P], words[:, u * P : (u + 1) * P], ident[:])
+            return bank
 
-        def copy_out(i0, i1, h, b, copy):
+        def copy_turned(i0, i1, h, bank):
             n = i1 - i0
-            dst = o_grp[h][:, i0 * P : i1 * P, :].rearrange("p m t -> p (m t)").bitcast(F32)
-            copy(
+            dst = out_mixed[h][:, i0 * P : i1 * P, :].rearrange("p m t -> p (m t)").bitcast(F32)
+            nc.scalar.copy(
                 out=dst.rearrange("p (a m u) -> p a m u", a=n, u=2),
-                in_=banks[b][:, 0 : 2 * n * P].rearrange("p (a u m) -> p a m u", a=n, u=2),
+                in_=bank[:, 0 : 2 * n * P].rearrange("p (a u m) -> p a m u", a=n, u=2),
             )
 
-        def out_quant(i0, i1, h):
-            quantize(o_codes[h], o_scales[:, h, :], o_grp[h], i0 * P, i1 * P)
-            if i1 < 3:
-                return
-            m0 = 3 * P if (h, i1) == (1, 4) else 0
-            dst = out_1[h].rearrange("p m t -> p (m t)").bitcast(I32)
-            nc.sync.dma_start(out=dst[:, m0 : i1 * P], in_=o_codes[h][:, m0 : i1 * P])
-            if (h, i1) == (1, 4):
-                rows_out = out_2.rearrange("g q m -> q g m").bitcast(I32)
-                for Q in range(4):
-                    queue = nc.scalar if Q < 2 else nc.sync
-                    queue.dma_start(
-                        out=rows_out[4 * Q : 4 * Q + 4, :, :], in_=o_scales[32 * Q : 32 * Q + 4, :, :].bitcast(I32)
-                    )
+        def quantize_out(i0, i1, h):
+            cols = slice(i0 * P, i1 * P)
+            quantize(out_words[h][:, cols], out_scales[:, h, cols], out_mixed[h][:, cols, :])
 
-        for step in ORDER:
-            kind = step[0:2]
-            a = [int(ch) for ch in step[2:]]
-            if kind == "PP":
-                permute_words(a[0])
-            elif kind == "SP":
-                permute_scales(a[0], a[1])
-            elif kind == "CV":
-                interleave("V", cb_grp[a[0], a[1]], cb_raw[a[0], a[1]], a[2])
-            elif kind == "CS":
-                interleave("S", cb_grp[a[0], a[1]], cb_raw[a[0], a[1]], a[2])
-            elif kind == "CQ":
-                quantize(cb_codes[a[0], a[1]], cb_scales[a[0], a[1]], cb_grp[a[0], a[1]], 0, W)
-            elif kind == "UU":
-                stage1(a[0], a[1], a[2:6])
-            elif kind == "IV":
-                interleave("V", grp[a[0], a[1]], rows[a[0], a[1]], a[2])
-            elif kind == "IS":
-                interleave("S", grp[a[0], a[1]], rows[a[0], a[1]], a[2])
-            elif kind == "QQ":
-                quantize(codes[a[0], a[1]], scales[a[0], a[1]], grp[a[0], a[1]], 0, W)
-            elif kind == "YY":
-                stage2(a[0], a[1], a[2], a[3], a[4])
-            elif kind == "AD":
-                add_rest(a[0], a[1], a[2])
-            elif kind == "AB":
-                add_round(a[0], a[1], a[2])
-            elif kind == "CA":
-                cast(a[0], a[1], nc.scalar.copy)
-            elif kind == "CW":
-                cast(a[0], a[1], nc.vector.tensor_copy)
-            elif kind == "TT":
-                turn(a[0], a[1], a[2], a[3])
-            elif kind == "CO":
-                copy_out(a[0], a[1], a[2], a[3], nc.scalar.copy)
-            elif kind == "CX":
-                copy_out(a[0], a[1], a[2], a[3], nc.vector.tensor_copy)
-            else:
-                out_quant(a[0], a[1], a[2])
+        def store_words(i0, i1, h):
+            dst = out_1[h].rearrange("p m t -> p (m t)").bitcast(I32)
+            nc.sync.dma_start(out=dst[:, i0 * P : i1 * P], in_=out_words[h][:, i0 * P : i1 * P])
+
+        on_vector, on_scalar = nc.vector.tensor_copy, nc.scalar.copy
+
+        reorder_words(0)
+        reorder_scales(0)
+        interleave_cb(on_scalar, 0, 0, W // 2, W)
+        interleave_cb(on_vector, 0, 0, 0, W // 2)
+        reorder_words(1)
+        build(SET_A, 0, bank_by_bank)
+        quantize_cb(0, 0, 1)
+        interleave_cb(on_vector, 0, 1, 0, W)
+        build(SET_A, 1, bank_by_bank)
+        quantize_cb(0, 1, 2)
+        build(SET_B0, 0, group_by_group)
+        reorder_words(2)
+        reorder_scales(1)
+        build(SET_A, 2, bank_by_bank)
+        interleave_unit(on_vector, SET_A, 0)
+        reorder_words(3)
+        build(SET_A, 3, bank_by_bank)
+        interleave_cb(on_vector, 1, 0, 0, W)
+        interleave_cb(on_vector, 1, 1, 0, W)
+        build(SET_B0, 1, bank_by_bank)
+        interleave_unit(on_vector, SET_A, 1)
+        quantize_cb(1, 0, 2)
+        build(SET_B0, 2, bank_by_bank)
+        interleave_unit(on_vector, SET_A, 2)
+        quantize_pair(0)
+        build(SET_B0, 3, bank_by_bank)
+        interleave_unit(on_vector, SET_A, 3)
+        interleave_unit(on_vector, SET_B0, 0)
+        quantize_pair(1)
+        build(SET_B1, 0, bank_by_bank)
+        interleave_unit(on_vector, SET_B0, 1)
+        interleave_unit(on_vector, SET_B0, 2)
+        quantize_pair(2)
+        build(SET_B1, 3, bank_by_bank)
+        interleave_unit(on_vector, SET_B0, 3)
+        build(SET_B1, 1, bank_by_bank)
+        interleave_unit(on_vector, SET_B1, 0)
+        quantize_pair(3)
+        build(SET_B1, 2, bank_by_bank)
+        interleave_unit(on_vector, SET_B1, 1)
+        quantize_unit(SET_B1, 0)
+        interleave_unit(on_scalar, SET_B1, 3)
+        interleave_unit(on_vector, SET_B1, 2)
+        for chunk in range(1, CHUNKS):
+            quantize_unit(SET_B1, chunk)
+
+        last = tiles[-1]
+        sums = {ih: contract(ih[0], ih[1], 0, W) for ih in tiles[:-1]}
+        for i, h in tiles[:-1]:
+            add_rest(i, h, sums[i, h], 0, W)
+            store_y(i, h)
+            if h == 0 or i == 0:
+                round_y(on_scalar, i, h)
+        turned = [turn(0, 2, 0), turn(2, 4, 0)]
+        round_y(on_vector, 1, 1)
+        round_y(on_vector, 2, 1)
+        copy_turned(0, 2, 0, turned[0])
+        copy_turned(2, 4, 0, turned[1])
+
+        halves = [(c0, c0 + W // 2) for c0 in (0, W // 2)]
+        last_sums = [contract(last[0], last[1], c0, c1) for c0, c1 in halves]
+        turned = [turn(0, 2, 1), turn(2, 3, 1)]
+        for acc, (c0, c1) in zip(last_sums, halves):
+            add_rest_rounded(last[0], last[1], acc, c0, c1)
+        quantize_out(0, 4, 0)
+        store_words(0, 4, 0)
+        copy_turned(0, 2, 1, turned[0])
+        turned_last = turn(3, 4, 1)
+        copy_turned(2, 3, 1, turned[1])
+        for acc, (c0, c1) in zip(last_sums, halves):
+            add_rest(last[0], last[1], acc, c0, c1)
+        store_y(last[0], last[1])
+        quantize_out(0, 2, 1)
+        copy_turned(3, 4, 1, turned_last)
+        quantize_out(2, 3, 1)
+        store_words(0, 3, 1)
+        quantize_out(3, 4, 1)
+        store_words(3, 4, 1)
+        scale_rows = out_2.rearrange("g q m -> q g m").bitcast(I32)
+        for Q in range(4):
+            queue = nc.scalar if Q < 2 else nc.sync
+            queue.dma_start(
+                out=scale_rows[4 * Q : 4 * Q + 4, :, :], in_=out_scales[32 * Q : 32 * Q + 4, :, :].bitcast(I32)
+            )

from contextlib import ExitStack

import concourse.mybir as mybir
from concourse.masks import make_identity

R, K, NA, NB = 2048, 1024, 512, 1024
FLOPS = 2 * R * K * (NA + NB) + 2 * R * NA * NB

F32 = mybir.dt.float32
BF16 = mybir.dt.bfloat16
I32 = mybir.dt.int32
U8 = mybir.dt.uint8
FP8X4 = mybir.dt.float8_e4m3fn_x4
FP4X4 = mybir.dt.float4_e2m1fn_x4
COPY = mybir.ActivationFunctionType.Copy
ADD = mybir.AluOpType.add

P = 128
W = 512
PACK = 4
CHUNKS = R // W
GROUPS = K // W
HALVES = NB // W
ROW_TILES = NA // P
BANKS = 8
SET_A, SET_B0, SET_B1 = 0, 1, 2
ROW_BUFS = 10
PAIR_BUFS = 3
WARM_BEFORE, WARM_AFTER = 14, 21


def tile_exchange_correlation_block_k4_kernel(
    tc, prim_words, prim_scales, coef_a_words, coef_a_scales, coef_b, quad, vxc, h_rest, out_0, out_1, out_2
):
    nc = tc.nc
    with ExitStack() as ctx:
        keep = ctx.enter_context(tc.tile_pool(name="keep", bufs=1))
        psum = ctx.enter_context(tc.psum_pool(name="psum", bufs=1))
        ctx.enter_context(tc.manual_schedule())

        def sb(name, shape, dtype):
            return keep.tile(shape, dtype, name=name, align_bytes=64)

        banks = [psum.tile([P, W], F32, name="bank%d" % b) for b in range(BANKS)]
        banks_taken = []

        def take_bank():
            banks_taken.append(1)
            return banks[(len(banks_taken) - 1) % BANKS]

        p_raw = [sb("p_raw%d" % c, [P, GROUPS, W], I32) for c in range(CHUNKS)]
        p_words = [sb("p_words%d" % c, [P, PACK, GROUPS, P], I32) for c in range(CHUNKS)]
        ps_raw = [sb("ps_raw%d" % part, [P, GROUPS, 2 * W // 4], I32) for part in range(2)]
        p_scales = [sb("p_scales%d" % part, [P, PACK, GROUPS, 2 * P // 4], I32) for part in range(2)]
        ca_words = sb("ca_words", [P, GROUPS, 2 * NA], U8)
        ca_scales = sb("ca_scales", [P, GROUPS, NA], U8)
        cb_raw = {(h, g): sb("cb_raw%d%d" % (h, g), [P, PACK, W], BF16) for h in range(HALVES) for g in range(GROUPS)}
        cb_mixed = [sb("cb_mixed%d" % h, [P, GROUPS * W, PACK], BF16) for h in range(HALVES)]
        cb_words = [sb("cb_words%d" % h, [P, GROUPS * W], I32) for h in range(HALVES)]
        cb_scales = [sb("cb_scales%d" % h, [P, GROUPS * W], U8) for h in range(HALVES)]
        rest = [sb("rest%d" % h, [P, ROW_TILES, W], BF16) for h in range(HALVES)]
        factor_raw = sb("factor_raw", [2 * CHUNKS, W], BF16)
        factor_rows = sb("factor_rows", [P, W], F32)
        factor = sb("factor", [P, 2 * CHUNKS, PACK], F32)
        ident = sb("ident", [P, P], F32)
        warm_in = sb("warm_in", [P, W], BF16)
        warm_words = sb("warm_words", [P, P], I32)
        warm_scales = sb("warm_scales", [P, P], U8)
        unit_rows = [sb("unit_rows%d" % n, [P, PACK, W], BF16) for n in range(ROW_BUFS)]
        pair_mixed = [sb("pair_mixed%d" % n, [P, 2 * W, PACK], BF16) for n in range(PAIR_BUFS)]
        pair_words = [sb("pair_words%d" % n, [P, 2 * W], I32) for n in range(3 * CHUNKS // 2)]
        pair_scales = [sb("pair_scales%d" % n, [P, 2 * W], U8) for n in range(3 * CHUNKS // 2)]
        tiles = [(i, h) for h in range(HALVES) for i in range(ROW_TILES)]
        y_f32 = {ih: sb("y_f32_%d%d" % ih, [P, W], F32) for ih in tiles}
        y_bf16 = {ih: sb("y_bf16_%d%d" % ih, [P, W], BF16) for ih in tiles}
        out_mixed = [sb("out_mixed%d" % h, [P, NA, PACK], BF16) for h in range(HALVES)]
        out_words = [sb("out_words%d" % h, [P, NA], I32) for h in range(HALVES)]
        out_scales = sb("out_scales", [P, HALVES, NA], U8)

        nc.gpsimd.memset(ps_raw[0][:], 0)
        make_identity(nc, ident[:])
        nc.vector.memset(warm_in[:], 0.0)
        nc.vector.memset(ca_scales[:].rearrange("p g n -> p (g n)").bitcast(I32), 0)
        nc.vector.quantize_mx(out=warm_words[:].bitcast(FP8X4), scales=warm_scales[:], in_=warm_in[:])
        nc.vector.memset(factor_rows[:], 0.0)
        nc.vector.memset(ps_raw[1][:], 0)

        prim_words_hbm = prim_words.rearrange("g p n t -> p g (n t)").bitcast(I32)
        prim_scales_hbm = prim_scales.rearrange("g q n -> q g n").bitcast(I32)
        ca_scales_hbm = coef_a_scales.rearrange("g q n -> q g n").bitcast(I32)

        def load_p(chunk):
            nc.sync.dma_start(out=p_raw[chunk][:], in_=prim_words_hbm[:, :, chunk * W : (chunk + 1) * W])

        def load_p_scales(part, quadrants):
            cols = slice(part * 2 * W // 4, (part + 1) * 2 * W // 4)
            for Q in quadrants:
                nc.sync.dma_start(
                    out=ps_raw[part][32 * Q : 32 * Q + 4, :, :], in_=prim_scales_hbm[4 * Q : 4 * Q + 4, :, cols]
                )

        def load_cb(h, g):
            src = coef_b[g * W : (g + 1) * W, h * W : (h + 1) * W]
            nc.sync.dma_start(out=cb_raw[h, g][:], in_=src.rearrange("(p t) n -> p t n", t=PACK))

        nc.sync.dma_start(out=factor_raw[0:CHUNKS, :], in_=quad.rearrange("(c n) -> c n", c=CHUNKS))
        nc.sync.dma_start(out=factor_raw[CHUNKS : 2 * CHUNKS, :], in_=vxc.rearrange("(c n) -> c n", c=CHUNKS))
        load_p_scales(0, (0, 1))
        nc.sync.dma_start(out=ca_words[:].bitcast(I32), in_=coef_a_words.rearrange("g p n -> p g n").bitcast(I32))
        load_p(0)
        load_p_scales(0, (2, 3))
        for Q in range(4):
            nc.sync.dma_start(
                out=ca_scales[32 * Q : 32 * Q + 4, :, :].bitcast(I32), in_=ca_scales_hbm[4 * Q : 4 * Q + 4, :, :]
            )
        load_cb(0, 0)
        load_p(1)
        load_cb(0, 1)
        load_p_scales(1, (0, 1, 2, 3))
        load_p(2)
        load_p(3)
        load_cb(1, 0)
        load_cb(1, 1)
        for h in range(HALVES):
            src = h_rest[:, h * W : (h + 1) * W]
            nc.sync.dma_start(out=rest[h][:], in_=src.rearrange("(i p) j -> p i j", p=P))

        def warm_up(count):
            for n in range(count):
                nc.tensor.matmul_mx(
                    out=banks[7][:, 0:P],
                    lhsT=warm_words[:].bitcast(FP8X4),
                    lhsT_scale=warm_scales[:],
                    rhs=warm_words[:].bitcast(FP8X4),
                    rhs_scale=warm_scales[:],
                    start=True,
                    stop=True,
                )

        warm_up(WARM_BEFORE)
        nc.scalar.activation(
            out=factor_rows[0 : 2 * CHUNKS, :].rearrange("v (t q e) -> v t q e", t=PACK, e=8),
            in_=factor_raw[:].rearrange("v (q t e) -> v t q e", t=PACK, e=8),
            func=COPY,
        )
        for t in range(PACK):
            nc.tensor.transpose(banks[6][:, t * P : (t + 1) * P], factor_rows[:, t * P : (t + 1) * P], ident[:])
        warm_up(WARM_AFTER)
        nc.scalar.activation(
            out=factor[:].rearrange("p v t -> p t v"),
            in_=banks[6][:].rearrange("p (t v) -> p t v", t=PACK)[:, :, 0 : 2 * CHUNKS],
            func=COPY,
        )

        def reorder_words(chunk):
            nc.vector.tensor_copy(
                out=p_words[chunk][:].rearrange("p t g (q e) -> p t (g q) e", e=8),
                in_=p_raw[chunk][:].rearrange("p g (q t e) -> p t (g q) e", t=PACK, e=8),
            )

        def reorder_scales(part):
            nc.vector.tensor_copy(
                out=p_scales[part][:].rearrange("p t g (b e) -> p t (g b) e", e=2),
                in_=ps_raw[part][:].rearrange("p g (b t e) -> p t (g b) e", t=PACK, e=2),
            )

        def interleave(copy, mixed, rows):
            copy(
                out=mixed.rearrange("p (c i) t -> p c t i", i=4),
                in_=rows.rearrange("p t (c i) -> p c t i", i=4),
            )

        def quantize(words, scales, mixed):
            nc.vector.quantize_mx(out=words.bitcast(FP8X4), scales=scales, in_=mixed.rearrange("p w t -> p (w t)"))

        def interleave_cb(copy, h, g, c0, c1):
            interleave(copy, cb_mixed[h][:, g * W + c0 : g * W + c1, :], cb_raw[h, g][:, :, c0:c1])

        def quantize_cb(h, g0, g1):
            cols = slice(g0 * W, g1 * W)
            quantize(cb_words[h][:, cols], cb_scales[h][:, cols], cb_mixed[h][:, cols, :])

        def unit_place(panel, chunk):
            n = CHUNKS * panel + chunk
            return n // 2, slice(n % 2 * W, (n % 2 + 1) * W)

        def build(panel, chunk, passes):
            rows = unit_rows[(CHUNKS * panel + chunk) % ROW_BUFS]
            v = chunk if panel == SET_A else CHUNKS + chunk
            slot_banks = [take_bank() for t in range(PACK)]
            for t, g in passes:
                if panel == SET_A:
                    rhs, rhs_scale = ca_words[:, g, :].bitcast(FP4X4), ca_scales[:, g, :]
                else:
                    cols = slice(g * W, (g + 1) * W)
                    rhs, rhs_scale = cb_words[panel - 1][:, cols].bitcast(FP8X4), cb_scales[panel - 1][:, cols]
                nc.tensor.matmul_mx(
                    out=slot_banks[t][:],
                    lhsT=p_words[chunk][:, t, g, :].bitcast(FP8X4),
                    lhsT_scale=p_scales[chunk // 2][:, t, g, 32 * (chunk % 2) : 32 * (chunk % 2 + 1)].bitcast(U8),
                    rhs=rhs,
                    rhs_scale=rhs_scale,
                    start=(g == 0),
                    stop=(g == GROUPS - 1),
                )
                if g == GROUPS - 1:
                    nc.scalar.activation(
                        out=rows[:, t, :], in_=slot_banks[t][:], func=COPY, scale=factor[:, v, t : t + 1]
                    )

        bank_by_bank = [(t, g) for t in range(PACK) for g in range(GROUPS)]
        group_by_group = [(t, g) for g in range(GROUPS) for t in range(PACK)]

        def interleave_unit(copy, panel, chunk):
            pair, cols = unit_place(panel, chunk)
            rows = unit_rows[(CHUNKS * panel + chunk) % ROW_BUFS]
            interleave(copy, pair_mixed[pair % PAIR_BUFS][:, cols, :], rows[:])

        def quantize_unit(panel, chunk):
            pair, cols = unit_place(panel, chunk)
            quantize(pair_words[pair][:, cols], pair_scales[pair][:, cols], pair_mixed[pair % PAIR_BUFS][:, cols, :])

        def quantize_pair(pair):
            quantize(pair_words[pair][:], pair_scales[pair][:], pair_mixed[pair % PAIR_BUFS][:])

        def contract(i, h, c0, c1):
            acc = take_bank()[:, 0 : c1 - c0]
            for chunk in range(CHUNKS):
                a_pair, a_cols = unit_place(SET_A, chunk)
                b_pair, b_cols = unit_place(SET_B0 + h, chunk)
                a_cols = slice(a_cols.start + i * P, a_cols.start + (i + 1) * P)
                b_cols = slice(b_cols.start + c0, b_cols.start + c1)
                nc.tensor.matmul_mx(
                    out=acc,
                    lhsT=pair_words[a_pair][:, a_cols].bitcast(FP8X4),
                    lhsT_scale=pair_scales[a_pair][:, a_cols],
                    rhs=pair_words[b_pair][:, b_cols].bitcast(FP8X4),
                    rhs_scale=pair_scales[b_pair][:, b_cols],
                    start=(chunk == 0),
                    stop=(chunk == CHUNKS - 1),
                )
            return acc

        def add_rest(i, h, acc, c0, c1):
            nc.vector.tensor_tensor(out=y_f32[i, h][:, c0:c1], in0=acc, in1=rest[h][:, i, c0:c1], op=ADD)

        def store_y(i, h):
            nc.sync.dma_start(out=out_0[i * P : (i + 1) * P, h * W : (h + 1) * W], in_=y_f32[i, h][:])

        def round_y(copy, i, h):
            copy(
                out=y_bf16[i, h][:].rearrange("p (u m e) -> p u m e", u=2, e=2),
                in_=y_f32[i, h][:].rearrange("p (m u e) -> p u m e", u=2, e=2),
            )

        def add_rest_rounded(i, h, acc, c0, c1):
            nc.vector.tensor_tensor(
                out=y_bf16[i, h][:].rearrange("p (u m e) -> p u m e", u=2, e=2)[:, :, c0 // PACK : c1 // PACK, :],
                in0=acc.rearrange("p (m u e) -> p u m e", u=2, e=2),
                in1=rest[h][:, i, c0:c1].rearrange("p (m u e) -> p u m e", u=2, e=2),
                op=ADD,
            )

        def turn(i0, i1, h):
            bank = take_bank()
            for i in range(i0, i1):
                words = y_bf16[i, h][:].bitcast(F32)
                for u in range(2):
                    s = 2 * (i - i0) + u
                    nc.tensor.transpose(bank[:, s * P : (s + 1) * P], words[:, u * P : (u + 1) * P], ident[:])
            return bank

        def copy_turned(i0, i1, h, bank):
            n = i1 - i0
            dst = out_mixed[h][:, i0 * P : i1 * P, :].rearrange("p m t -> p (m t)").bitcast(F32)
            nc.scalar.copy(
                out=dst.rearrange("p (a m u) -> p a m u", a=n, u=2),
                in_=bank[:, 0 : 2 * n * P].rearrange("p (a u m) -> p a m u", a=n, u=2),
            )

        def quantize_out(i0, i1, h):
            cols = slice(i0 * P, i1 * P)
            quantize(out_words[h][:, cols], out_scales[:, h, cols], out_mixed[h][:, cols, :])

        def store_words(i0, i1, h):
            dst = out_1[h].rearrange("p m t -> p (m t)").bitcast(I32)
            nc.sync.dma_start(out=dst[:, i0 * P : i1 * P], in_=out_words[h][:, i0 * P : i1 * P])

        on_vector, on_scalar = nc.vector.tensor_copy, nc.scalar.copy

        reorder_words(0)
        reorder_scales(0)
        interleave_cb(on_scalar, 0, 0, W // 2, W)
        interleave_cb(on_vector, 0, 0, 0, W // 2)
        reorder_words(1)
        build(SET_A, 0, bank_by_bank)
        quantize_cb(0, 0, 1)
        interleave_cb(on_vector, 0, 1, 0, W)
        build(SET_A, 1, bank_by_bank)
        quantize_cb(0, 1, 2)
        build(SET_B0, 0, group_by_group)
        reorder_words(2)
        reorder_scales(1)
        build(SET_A, 2, bank_by_bank)
        interleave_unit(on_vector, SET_A, 0)
        reorder_words(3)
        build(SET_A, 3, bank_by_bank)
        interleave_cb(on_vector, 1, 0, 0, W)
        interleave_cb(on_vector, 1, 1, 0, W)
        build(SET_B0, 1, bank_by_bank)
        interleave_unit(on_vector, SET_A, 1)
        quantize_cb(1, 0, 2)
        build(SET_B0, 2, bank_by_bank)
        interleave_unit(on_vector, SET_A, 2)
        quantize_pair(0)
        build(SET_B0, 3, bank_by_bank)
        interleave_unit(on_vector, SET_A, 3)
        interleave_unit(on_vector, SET_B0, 0)
        quantize_pair(1)
        build(SET_B1, 0, bank_by_bank)
        interleave_unit(on_vector, SET_B0, 1)
        interleave_unit(on_vector, SET_B0, 2)
        quantize_pair(2)
        build(SET_B1, 3, bank_by_bank)
        interleave_unit(on_vector, SET_B0, 3)
        build(SET_B1, 1, bank_by_bank)
        interleave_unit(on_vector, SET_B1, 0)
        quantize_pair(3)
        build(SET_B1, 2, bank_by_bank)
        interleave_unit(on_vector, SET_B1, 1)
        quantize_unit(SET_B1, 0)
        interleave_unit(on_scalar, SET_B1, 3)
        interleave_unit(on_vector, SET_B1, 2)
        for chunk in range(1, CHUNKS):
            quantize_unit(SET_B1, chunk)

        last = tiles[-1]
        sums = {ih: contract(ih[0], ih[1], 0, W) for ih in tiles[:-1]}
        for i, h in tiles[:-1]:
            add_rest(i, h, sums[i, h], 0, W)
            store_y(i, h)
            if h == 0 or i == 0:
                round_y(on_scalar, i, h)
        turned = [turn(0, 2, 0), turn(2, 4, 0)]
        round_y(on_vector, 1, 1)
        round_y(on_vector, 2, 1)
        copy_turned(0, 2, 0, turned[0])
        copy_turned(2, 4, 0, turned[1])

        halves = [(c0, c0 + W // 2) for c0 in (0, W // 2)]
        last_sums = [contract(last[0], last[1], c0, c1) for c0, c1 in halves]
        turned = [turn(0, 2, 1), turn(2, 3, 1)]
        for acc, (c0, c1) in zip(last_sums, halves):
            add_rest_rounded(last[0], last[1], acc, c0, c1)
        quantize_out(0, 4, 0)
        store_words(0, 4, 0)
        copy_turned(0, 2, 1, turned[0])
        turned_last = turn(3, 4, 1)
        copy_turned(2, 3, 1, turned[1])
        for acc, (c0, c1) in zip(last_sums, halves):
            add_rest(last[0], last[1], acc, c0, c1)
        store_y(last[0], last[1])
        quantize_out(0, 2, 1)
        copy_turned(3, 4, 1, turned_last)
        quantize_out(2, 3, 1)
        store_words(0, 3, 1)
        quantize_out(3, 4, 1)
        store_words(3, 4, 1)
        scale_rows = out_2.rearrange("g q m -> q g m").bitcast(I32)
        for Q in range(4):
            queue = nc.scalar if Q < 2 else nc.sync
            queue.dma_start(
                out=scale_rows[4 * Q : 4 * Q + 4, :, :], in_=out_scales[32 * Q : 32 * Q + 4, :, :].bitcast(I32)
            )
